import numpy as np
CORES = [0,1,2,3]
N = 4
T = 512
ROUTE = [[[2,1],[2,0],[2,0],[3,1],[2,1],[1,2],[2,0],[2,3],[3,2],[2,3],[1,2],[1,3],[0,3],[1,3],[0,3],[2,3],[3,2],[3,1],[3,2],[3,0],[2,1],[3,0],[0,3],[2,1],[1,2],[1,2],[0,3],[3,2],[0,2],[0,1],[3,2],[1,2],[2,0],[1,2],[2,3],[0,2],[0,2],[2,3],[3,0],[1,2],[3,2],[2,1],[2,3],[2,3],[1,2],[0,2],[2,0],[2,3],[2,3],[2,3],[2,1],[2,3],[2,3],[2,3],[2,0],[2,3],[2,3],[2,1],[1,0],[2,3],[2,0],[2,3],[3,2],[1,3],[2,1],[0,3],[2,1],[2,0],[2,3],[0,2],[2,3],[0,1],[3,1],[2,1],[3,1],[3,2],[1,2],[2,3],[1,2],[2,1],[0,2],[0,2],[0,3],[3,2],[0,1],[2,3],[0,2],[0,2],[2,0],[1,2],[2,0],[0,2],[2,1],[2,0],[2,1],[1,2],[1,2],[2,3],[2,3],[2,1],[2,3],[2,3],[2,0],[2,1],[2,0],[2,1],[2,0],[0,1],[2,3],[3,1],[2,0],[0,2],[0,3],[2,3],[1,2],[1,2],[2,3],[3,2],[1,2],[3,2],[3,0],[2,0],[1,2],[2,1],[2,3],[2,0],[1,2],[2,0],[2,1],[2,0],[0,2],[2,1],[1,2],[2,1],[2,1],[1,2],[0,2],[2,3],[3,2],[0,2],[2,0],[0,3],[2,3],[3,2],[2,0],[2,3],[2,0],[0,1],[2,3],[1,3],[1,2],[0,1],[2,3],[0,3],[3,2],[2,3],[2,3],[0,2],[0,2],[2,3],[2,3],[3,1],[2,0],[2,1],[0,2],[1,3],[2,0],[2,3],[2,0],[2,0],[1,2],[2,0],[2,1],[3,2],[2,1],[1,2],[0,2],[2,3],[2,1],[2,0],[2,3],[2,0],[2,3],[3,1],[3,2],[0,2],[0,2],[0,2],[2,0],[3,2],[2,3],[2,0],[3,2],[2,0],[2,1],[1,2],[2,1],[1,2],[2,3],[2,3],[3,0],[2,1],[0,2],[3,2],[1,3],[2,3],[2,3],[2,1],[1,3],[2,1],[2,3],[0,2],[2,3],[1,2],[2,3],[2,3],[0,2],[3,2],[2,3],[0,1],[3,2],[2,3],[1,2],[1,2],[0,2],[1,2],[0,3],[2,3],[1,3],[2,0],[0,2],[2,0],[0,2],[2,1],[2,3],[0,2],[2,3],[1,2],[2,1],[2,1],[3,0],[2,0],[2,0],[2,0],[2,1],[1,2],[2,1],[3,0],[3,1],[2,1],[0,2],[2,1],[0,3],[2,1],[2,3],[2,1],[1,2],[0,3],[2,3],[3,1],[0,1],[2,3],[0,2],[1,2],[0,3],[2,0],[2,3],[1,3],[1,2],[2,1],[3,2],[1,2],[2,0],[2,3],[0,2],[2,3],[2,1],[2,0],[2,0],[2,0],[3,1],[2,3],[1,2],[2,0],[2,1],[2,3],[0,2],[2,3],[1,3],[2,0],[2,0],[0,2],[2,3],[1,2],[2,3],[2,3],[1,3],[2,3],[2,0],[2,3],[2,0],[2,3],[2,0],[3,2],[2,0],[2,0],[2,3],[1,2],[2,0],[2,3],[2,3],[2,1],[2,1],[0,2],[2,0],[2,3],[1,3],[2,0],[1,2],[2,1],[2,3],[1,2],[0,2],[1,2],[1,0],[2,0],[2,3],[2,1],[2,0],[2,1],[2,0],[0,2],[2,3],[2,0],[0,2],[2,3],[1,3],[3,0],[1,2],[3,2],[2,3],[2,0],[2,1],[0,2],[3,2],[2,3],[0,2],[2,0],[3,2],[2,1],[0,2],[2,3],[2,3],[2,0],[0,2],[3,1],[3,2],[2,0],[2,0],[3,2],[2,0],[0,2],[3,2],[1,2],[0,2],[3,2],[0,3],[2,3],[2,3],[3,2],[3,2],[1,0],[2,0],[0,2],[2,1],[2,1],[2,0],[1,2],[2,3],[1,2],[2,1],[2,1],[0,2],[0,2],[1,2],[0,2],[2,3],[0,2],[1,3],[0,1],[3,2],[2,1],[2,0],[2,0],[0,3],[1,3],[0,2],[1,2],[2,0],[1,2],[3,1],[2,3],[3,1],[0,2],[3,2],[3,2],[3,2],[2,3],[1,2],[0,2],[1,2],[0,3],[2,0],[3,2],[2,1],[3,0],[2,1],[2,1],[1,2],[1,2],[3,0],[2,1],[2,3],[2,0],[2,0],[2,1],[1,2],[2,3],[1,3],[2,0],[0,2],[2,1],[3,2],[3,2],[0,2],[3,2],[0,2],[2,0],[2,1],[3,0],[2,0],[3,2],[0,3],[2,0],[3,2],[1,2],[2,1],[0,2],[2,0],[2,1],[3,2],[2,3],[0,3],[0,3],[1,2],[2,1],[3,2],[0,2],[2,0],[2,0],[0,3],[2,3],[2,1],[2,3],[2,1],[3,1],[2,3],[2,3],[1,3],[1,3],[2,1],[2,3],[2,1],[2,0],[2,1],[2,1],[0,3],[2,0],[3,2],[1,2],[2,3],[2,0],[1,2],[2,3],[3,2],[2,3],[3,2],[1,2],[3,1],[3,0],[2,0],[2,0],[2,0],[0,2],[3,0],[2,3],[3,0],[2,0],[2,0],[2,1],[3,1],[2,3],[0,2],[1,2],[2,0],[2,1],[1,3],[1,3],[2,3],[0,1],[0,2],[2,1]],[[2,3],[2,0],[0,2],[2,1],[0,2],[2,3],[1,2],[2,1],[1,2],[1,3],[2,1],[2,0],[2,1],[0,2],[2,1],[2,0],[2,0],[1,2],[2,3],[1,2],[2,1],[2,0],[2,0],[0,3],[1,2],[2,1],[2,3],[2,1],[2,0],[2,3],[0,1],[0,2],[1,0],[2,0],[2,3],[1,3],[1,2],[0,2],[2,3],[2,0],[2,0],[3,2],[2,3],[2,1],[2,3],[0,2],[2,3],[2,3],[0,2],[2,0],[2,1],[2,1],[3,1],[2,3],[2,1],[2,0],[0,3],[1,2],[2,1],[1,2],[2,1],[3,2],[2,3],[1,2],[3,0],[3,2],[2,1],[2,0],[2,1],[2,1],[1,3],[2,1],[2,3],[2,0],[2,3],[2,3],[2,1],[1,2],[2,0],[2,3],[3,0],[3,1],[2,1],[2,1],[2,1],[0,1],[2,1],[0,2],[2,0],[0,2],[2,1],[2,3],[3,0],[3,0],[1,0],[2,0],[2,1],[2,0],[2,3],[2,3],[2,1],[2,3],[0,1],[2,0],[2,3],[0,2],[0,2],[2,0],[2,3],[2,0],[3,1],[2,0],[2,0],[1,2],[2,0],[2,3],[2,0],[3,2],[2,3],[2,3],[0,2],[2,0],[1,2],[0,1],[0,2],[2,0],[3,2],[0,3],[0,1],[2,0],[1,2],[1,2],[2,0],[0,2],[2,0],[3,2],[3,2],[2,3],[1,2],[2,3],[3,2],[2,3],[2,1],[2,1],[2,3],[2,0],[2,1],[2,0],[2,3],[2,3],[1,3],[2,0],[2,0],[0,2],[1,3],[2,1],[2,1],[1,2],[2,1],[2,1],[0,2],[2,1],[1,3],[0,2],[2,0],[2,3],[2,0],[2,1],[2,0],[2,1],[3,2],[2,0],[0,2],[1,3],[1,3],[2,3],[2,3],[2,0],[2,1],[2,1],[0,1],[0,1],[2,0],[2,1],[2,3],[1,3],[0,2],[0,2],[2,1],[2,1],[2,3],[2,3],[3,2],[3,2],[2,0],[3,2],[2,1],[2,1],[3,2],[2,0],[1,0],[3,2],[2,0],[1,2],[1,3],[3,2],[3,2],[2,1],[2,3],[3,2],[0,2],[2,0],[2,3],[0,3],[1,2],[2,0],[2,0],[2,0],[2,3],[3,2],[2,1],[2,1],[0,2],[2,3],[1,2],[1,2],[1,0],[3,2],[0,1],[2,1],[2,0],[3,2],[2,0],[0,1],[2,1],[0,2],[2,0],[2,3],[3,2],[3,2],[3,2],[2,0],[0,2],[2,3],[2,3],[0,2],[2,0],[3,2],[2,3],[0,2],[2,1],[2,1],[2,0],[0,2],[2,1],[2,0],[2,1],[3,2],[1,2],[2,0],[0,2],[2,1],[1,0],[2,1],[1,2],[2,0],[2,1],[1,2],[0,3],[3,2],[2,0],[2,0],[3,0],[2,3],[1,2],[2,0],[0,1],[3,2],[0,3],[2,3],[2,1],[2,0],[2,0],[2,3],[2,1],[1,0],[2,1],[2,1],[2,1],[0,2],[2,3],[2,3],[2,3],[2,1],[2,1],[2,1],[2,0],[2,0],[0,1],[2,0],[0,2],[0,2],[2,1],[2,0],[0,2],[1,2],[2,0],[0,2],[3,2],[1,2],[1,0],[2,3],[2,3],[2,0],[2,0],[3,1],[1,2],[2,0],[2,0],[2,1],[2,1],[2,3],[2,1],[0,2],[2,3],[1,2],[2,1],[3,1],[3,2],[1,2],[2,3],[2,1],[2,3],[2,3],[0,2],[2,1],[2,0],[3,0],[2,3],[2,3],[2,1],[2,1],[2,1],[2,3],[2,1],[2,3],[2,0],[1,0],[2,0],[1,3],[1,2],[0,1],[3,2],[2,1],[1,2],[2,0],[2,3],[2,1],[1,2],[3,1],[1,2],[0,2],[2,0],[1,2],[3,1],[2,1],[3,0],[3,1],[3,1],[2,1],[2,0],[1,2],[2,1],[1,2],[2,0],[2,3],[2,3],[2,0],[3,2],[3,2],[1,3],[2,0],[2,3],[2,1],[1,0],[0,3],[2,3],[2,3],[2,1],[2,0],[0,1],[0,2],[0,3],[2,3],[2,1],[0,1],[2,3],[2,0],[0,2],[1,0],[2,0],[2,3],[3,2],[2,0],[2,1],[3,2],[2,0],[3,2],[2,0],[3,1],[3,2],[2,3],[1,0],[2,1],[2,0],[2,3],[2,1],[2,0],[1,2],[0,2],[2,0],[2,1],[2,3],[2,3],[2,3],[0,2],[2,0],[0,1],[2,3],[1,2],[1,0],[0,2],[2,3],[0,2],[2,0],[1,0],[0,2],[0,2],[3,2],[2,0],[3,2],[2,1],[3,2],[2,3],[2,0],[3,2],[2,0],[0,2],[2,3],[2,3],[3,2],[0,3],[2,3],[1,0],[2,1],[0,2],[3,2],[0,1],[2,1],[3,2],[2,1],[2,1],[3,2],[3,2],[2,1],[3,2],[3,2],[2,0],[2,3],[3,2],[2,1],[2,1],[3,2],[1,2],[2,3],[2,3],[2,0],[2,1],[2,1],[2,1],[3,0],[3,2],[3,2],[0,2],[0,1],[2,0],[0,1],[2,3],[1,2],[3,1],[3,1],[3,2],[2,0],[0,3],[2,0],[0,2],[0,3],[1,2],[2,3],[2,1],[2,3],[2,0],[2,0],[0,2],[2,1],[2,1],[2,0],[1,2],[0,2],[0,3],[2,1],[2,0]],[[2,3],[2,1],[2,3],[3,2],[2,3],[2,3],[1,3],[2,0],[1,0],[0,3],[1,2],[2,1],[2,0],[0,2],[1,3],[0,3],[2,1],[2,1],[2,1],[2,0],[3,1],[3,2],[2,3],[2,3],[0,2],[2,1],[1,2],[1,2],[3,1],[3,2],[3,2],[0,2],[2,3],[2,3],[2,0],[3,2],[2,1],[2,1],[3,2],[2,3],[3,2],[2,0],[0,2],[0,1],[3,2],[2,0],[2,3],[0,3],[2,0],[1,2],[2,1],[0,1],[3,2],[2,1],[3,2],[2,3],[3,2],[2,0],[2,1],[3,1],[2,0],[1,2],[2,0],[2,0],[2,3],[2,3],[0,3],[1,2],[2,1],[0,2],[3,1],[2,0],[2,0],[2,3],[2,3],[2,0],[0,2],[2,0],[2,3],[2,3],[0,1],[2,3],[2,1],[1,0],[0,2],[1,2],[3,1],[2,3],[2,0],[2,0],[0,2],[0,2],[3,0],[0,2],[3,1],[1,3],[2,0],[2,0],[1,2],[2,3],[2,0],[1,2],[3,2],[2,0],[3,2],[1,0],[2,1],[2,1],[1,2],[2,3],[3,2],[3,2],[0,1],[2,1],[2,0],[1,2],[2,0],[1,2],[2,1],[1,2],[2,1],[2,1],[1,0],[2,0],[3,1],[2,0],[2,1],[2,0],[1,3],[1,2],[2,1],[2,1],[3,2],[2,0],[2,0],[2,0],[2,1],[2,1],[2,0],[3,2],[2,0],[0,3],[3,1],[2,0],[2,3],[2,0],[1,3],[0,3],[3,2],[1,2],[2,1],[2,0],[1,2],[1,0],[2,0],[3,1],[2,1],[2,3],[0,2],[3,2],[3,2],[2,3],[1,2],[2,1],[2,0],[2,1],[0,2],[3,2],[1,2],[2,1],[3,0],[0,3],[0,2],[3,2],[1,3],[2,3],[3,2],[3,2],[3,1],[3,1],[2,1],[1,2],[2,1],[2,0],[3,2],[0,1],[2,1],[2,3],[0,2],[3,2],[0,3],[3,0],[1,2],[2,0],[1,2],[2,3],[3,2],[2,0],[2,3],[2,0],[1,0],[2,3],[2,0],[2,1],[2,3],[1,2],[2,1],[3,1],[2,1],[2,1],[2,3],[3,1],[2,0],[1,2],[2,0],[1,3],[2,3],[2,0],[2,0],[3,2],[2,1],[2,0],[2,0],[0,2],[3,2],[2,3],[0,2],[2,3],[0,2],[2,0],[2,1],[2,0],[2,0],[0,3],[1,2],[2,0],[2,3],[2,0],[0,2],[2,3],[2,3],[1,2],[2,3],[1,2],[2,1],[3,2],[2,3],[3,2],[2,1],[2,1],[2,0],[2,1],[3,2],[2,3],[2,1],[2,3],[2,0],[1,2],[3,2],[2,0],[0,3],[2,0],[2,1],[2,3],[3,2],[2,1],[2,3],[0,2],[3,1],[3,2],[3,0],[2,3],[3,2],[3,0],[2,1],[2,0],[2,0],[0,2],[2,0],[2,1],[2,0],[0,2],[2,3],[0,2],[0,2],[2,0],[0,2],[0,3],[3,2],[3,2],[2,1],[2,3],[1,2],[2,3],[1,0],[2,0],[3,2],[1,3],[2,3],[1,0],[2,0],[2,3],[1,2],[1,2],[3,1],[0,2],[2,3],[1,0],[2,0],[2,1],[2,0],[1,2],[2,3],[2,1],[3,1],[1,3],[2,3],[3,0],[2,0],[2,3],[0,2],[1,3],[2,3],[2,3],[3,2],[0,2],[2,3],[0,2],[2,3],[0,2],[2,3],[2,3],[1,0],[3,2],[1,2],[2,3],[1,2],[3,0],[2,1],[2,0],[1,2],[2,0],[0,2],[2,3],[2,0],[3,2],[2,1],[1,2],[3,0],[3,0],[2,3],[2,3],[1,3],[1,2],[2,3],[2,3],[3,2],[2,1],[2,3],[0,3],[3,0],[3,2],[2,1],[0,2],[2,0],[2,3],[2,1],[0,2],[2,3],[2,1],[2,1],[0,2],[2,3],[3,2],[2,3],[0,2],[2,3],[0,2],[2,1],[2,1],[3,1],[3,2],[2,3],[2,3],[0,1],[2,3],[3,2],[2,3],[2,0],[2,3],[1,2],[2,3],[3,2],[3,2],[0,3],[2,3],[2,3],[3,2],[2,0],[0,2],[2,0],[1,3],[3,1],[0,2],[2,1],[1,3],[1,2],[2,3],[2,3],[2,3],[3,2],[1,2],[2,3],[2,0],[2,0],[2,0],[2,3],[2,3],[2,1],[2,3],[1,2],[2,1],[0,3],[2,3],[2,3],[2,3],[1,3],[0,2],[2,1],[2,0],[2,3],[2,0],[0,2],[3,2],[3,1],[2,1],[3,2],[2,3],[2,1],[3,1],[0,3],[2,0],[3,2],[3,2],[2,1],[3,1],[3,2],[2,3],[2,3],[2,1],[1,2],[2,0],[2,3],[1,2],[2,1],[1,0],[3,2],[2,3],[2,0],[2,1],[2,3],[2,1],[2,0],[2,1],[2,1],[0,2],[2,1],[2,1],[2,0],[1,3],[2,3],[2,3],[3,2],[0,2],[3,2],[1,0],[0,2],[2,3],[2,3],[2,3],[3,2],[3,2],[3,2],[2,0],[2,0],[2,1],[2,1],[3,2],[2,1],[2,0],[2,0],[2,1],[1,2],[1,2],[2,0],[2,1],[0,2],[2,3],[2,0],[2,3],[1,3],[3,2],[0,1],[2,3],[0,1],[2,0],[2,3],[2,1],[3,0],[2,1],[0,2],[2,0]],[[2,3],[2,1],[2,0],[2,0],[2,3],[3,2],[2,1],[1,2],[0,2],[2,3],[2,1],[2,1],[2,3],[3,0],[3,0],[2,3],[2,0],[2,0],[0,2],[2,3],[2,0],[3,2],[2,0],[0,2],[2,3],[3,2],[2,1],[2,3],[0,2],[2,0],[0,3],[2,1],[2,1],[0,2],[2,0],[2,0],[2,1],[2,3],[2,1],[2,0],[3,0],[2,1],[2,1],[0,2],[1,2],[0,1],[3,2],[3,2],[3,2],[1,0],[2,1],[2,3],[3,0],[1,2],[0,2],[2,3],[3,0],[1,2],[2,3],[1,2],[2,3],[2,0],[1,2],[2,3],[2,3],[2,1],[2,0],[2,3],[0,2],[2,1],[1,2],[1,3],[2,0],[0,1],[2,1],[1,3],[3,0],[2,1],[0,1],[2,1],[2,3],[2,1],[1,3],[1,2],[2,3],[1,0],[0,3],[2,0],[2,0],[2,3],[3,1],[2,3],[2,3],[1,2],[2,1],[0,3],[1,2],[2,0],[3,2],[2,3],[2,0],[3,2],[2,1],[0,1],[2,0],[2,1],[2,1],[0,2],[3,2],[3,0],[1,2],[2,3],[2,3],[2,3],[3,2],[2,1],[2,0],[2,1],[1,2],[1,3],[2,3],[2,3],[0,2],[1,2],[2,1],[2,0],[0,3],[3,2],[2,0],[1,2],[2,1],[2,0],[2,1],[1,2],[3,1],[3,0],[2,0],[2,1],[3,2],[2,3],[2,1],[2,0],[0,2],[2,3],[3,0],[2,3],[3,0],[2,0],[2,3],[2,0],[2,1],[2,0],[0,2],[3,0],[2,3],[3,2],[1,2],[2,0],[1,0],[2,3],[2,3],[3,0],[2,1],[2,3],[2,3],[2,1],[2,3],[3,2],[2,3],[0,2],[2,3],[3,2],[2,3],[2,1],[3,1],[2,3],[1,3],[2,1],[2,0],[0,2],[0,2],[2,1],[2,0],[1,0],[0,2],[2,1],[2,0],[0,3],[0,2],[2,1],[3,0],[1,2],[2,3],[1,0],[1,0],[2,0],[0,2],[1,0],[2,1],[2,1],[3,1],[0,2],[2,0],[2,3],[2,1],[2,0],[1,2],[2,1],[2,3],[2,0],[2,1],[2,3],[1,2],[1,3],[0,2],[1,3],[0,1],[2,0],[0,2],[2,3],[1,2],[0,1],[1,0],[1,2],[2,0],[2,1],[2,1],[2,0],[1,2],[2,1],[2,0],[2,3],[2,3],[2,3],[3,1],[2,3],[0,2],[2,3],[2,0],[0,1],[2,3],[2,1],[2,0],[0,2],[2,3],[2,1],[0,1],[3,2],[2,0],[3,2],[3,1],[2,3],[2,1],[2,1],[0,2],[2,3],[1,3],[3,2],[2,0],[3,2],[0,1],[3,1],[1,2],[2,3],[1,2],[0,3],[2,0],[2,3],[2,0],[2,3],[2,0],[2,3],[1,2],[1,2],[2,1],[1,2],[2,0],[0,2],[2,3],[2,3],[2,1],[2,3],[2,3],[2,1],[3,2],[2,1],[3,2],[2,3],[3,2],[1,2],[3,2],[2,3],[2,3],[2,1],[2,3],[3,1],[1,3],[2,0],[1,2],[2,3],[3,1],[2,3],[2,0],[2,0],[0,2],[2,3],[2,0],[2,3],[2,0],[2,1],[2,1],[2,0],[2,3],[2,3],[2,0],[0,2],[3,2],[0,2],[2,0],[2,1],[3,2],[0,3],[3,2],[2,3],[3,0],[2,0],[3,2],[3,2],[3,2],[2,3],[2,3],[1,2],[2,0],[3,1],[2,1],[3,1],[1,2],[2,1],[2,3],[1,2],[2,1],[3,2],[3,2],[1,2],[2,3],[0,2],[2,0],[2,0],[2,3],[2,3],[3,1],[0,2],[3,0],[2,3],[2,3],[0,2],[2,0],[2,3],[0,2],[2,0],[2,3],[3,1],[2,0],[2,1],[2,0],[3,2],[1,0],[2,0],[2,3],[0,2],[0,2],[2,1],[2,3],[1,2],[2,3],[2,1],[2,3],[2,1],[1,3],[2,0],[1,2],[0,2],[2,0],[2,0],[2,3],[1,2],[2,0],[0,1],[2,0],[0,2],[2,1],[2,0],[2,1],[1,0],[0,1],[3,2],[1,2],[3,2],[2,3],[3,0],[0,2],[2,0],[0,3],[2,3],[2,1],[3,2],[2,0],[2,0],[3,2],[2,3],[1,3],[2,3],[0,2],[1,0],[2,0],[1,0],[2,1],[2,1],[2,3],[2,1],[3,2],[3,2],[2,1],[1,2],[1,2],[2,0],[3,2],[2,0],[2,1],[2,1],[0,1],[1,2],[2,0],[1,3],[0,2],[2,0],[2,1],[3,1],[2,0],[2,1],[1,2],[2,3],[1,3],[2,3],[0,2],[2,0],[0,2],[0,3],[0,2],[1,2],[2,0],[2,0],[1,0],[0,2],[2,1],[1,0],[3,2],[2,3],[1,0],[2,0],[2,0],[0,3],[2,0],[2,0],[2,1],[2,1],[2,0],[0,2],[3,2],[1,2],[2,1],[2,0],[2,0],[2,3],[1,2],[2,0],[2,3],[2,3],[2,3],[1,2],[0,3],[2,0],[1,0],[2,1],[1,3],[0,2],[0,3],[0,3],[2,1],[0,2],[3,2],[2,1],[2,0],[0,2],[3,1],[2,3],[2,3],[0,2],[2,1],[2,0],[2,0],[2,3],[2,1],[2,3],[2,3],[2,0],[1,3],[2,3],[1,3],[2,0],[2,3],[3,2]]]
CAP = 1061
YW = 1061
def setup_inputs(rng):
    return {"x": rng.standard_normal((N, 128, T), dtype=np.float32)}
def reference(x):
    y = np.full((N, 128, YW), np.nan, x.dtype)
    fill = [0] * N
    for r in range(N):
        for t in range(T):
            for e in ROUTE[r][t]:
                if fill[e] < CAP:
                    y[e][:, fill[e]] = x[r][:, t]
                fill[e] += 1
    return {"y": y}

@@ -1,0 +1,92 @@
+SCRATCH = {
+    "xs": ("sbuf", [128, 512], "float32"),
+    "pack": ("sbuf", [128, 1024], "float32"),
+    "out": ("sbuf", [128, 1061], "float32"),
+}
+SEMAPHORES = ["ld", "pk0", "pk1", "pk2", "pk3", "gp0", "gp1", "gp2", "gp3", "arr", "sent", "st"]
+
+
+def plan(tables):
+    route, cap, n = tables["ROUTE"], tables["CAP"], len(tables["ROUTE"])
+    fill = [0] * n
+    kept = [[[] for _e in range(n)] for _r in range(n)]
+    off = [[0] * n for _r in range(n)]
+    for r in range(n):
+        for e in range(n):
+            off[r][e] = min(fill[e], cap)
+        for t, experts in enumerate(route[r]):
+            for e in experts:
+                if fill[e] < cap:
+                    kept[r][e].append(t)
+                fill[e] += 1
+    return kept, off, [min(f, cap) for f in fill]
+
+
+def runs_of(tokens):
+    runs = []
+    for pos, t in enumerate(tokens):
+        if runs and runs[-1][0] + runs[-1][1] == t:
+            runs[-1][1] += 1
+        else:
+            runs.append([t, 1, pos])
+    return runs
+
+
+def rank_program(g, core, T, topo):
+    rank = T.rank_of(core)
+    if rank is None:
+        return
+    kept, off, count = plan(T.tables)
+    n = len(T.cores)
+    S = T.sem
+    queues = [g.sync, g.scalar, g]
+
+    g.sync.dma_start(T.xs[:], T.x[:]).then_inc(S.ld, 16)
+    for q in queues:
+        q.wait_ge(S.ld, 16)
+
+    others = sorted((e for e in range(n) if e != rank and kept[rank][e]), key=lambda e: -len(kept[rank][e]))
+    order = others + ([rank] if kept[rank][rank] else [])
+    place, base = {}, 0
+    for e in others:
+        place[e] = (T.pack, base)
+        base += len(kept[rank][e])
+    place[rank] = (T.out, off[rank][rank])
+
+    share = {e: [runs_of(kept[rank][e])[k::3] for k in range(3)] for e in order}
+
+    def issue(k, e):
+        buf, b = place[e]
+        sem = S["gp%d" % e] if k == 2 else S["pk%d" % e]
+        for t, ln, pos in share[e][k]:
+            queues[k].dma_start(buf[:, b + pos:b + pos + ln], T.xs[:, t:t + ln]).then_inc(sem, 16)
+
+    for k in (0, 1):
+        for e in order:
+            issue(k, e)
+
+    if order:
+        issue(2, order[0])
+    for i, e in enumerate(order):
+        if i + 1 < len(order):
+            issue(2, order[i + 1])
+        hw = len(share[e][0]) + len(share[e][1])
+        if hw:
+            g.wait_ge(S["pk%d" % e], 16 * hw)
+        if share[e][2]:
+            g.wait_ge(S["gp%d" % e], 16 * len(share[e][2]))
+        if e != rank:
+            dst = T.cores[e]
+            rid, pid, _se = topo.addr(dst)
+            b, w = place[e][1], len(kept[rank][e])
+            g.remote_dma(T.out[:, off[rank][e]:off[rank][e] + w], T.pack[:, b:b + w], S.arr, S.sent,
+                         pid, rid, topo.mask(core, dst))
+
+    senders = sum(1 for r in range(n) if r != rank and kept[r][rank])
+    if senders:
+        g.wait_ge(S.arr, 16 * senders)
+    if count[rank]:
+        g.dma_start(T.y[:, 0:count[rank]], T.out[:, 0:count[rank]]).then_inc(S.st, 16)
+        g.wait_ge(S.st, 16)
+    if others:
+        g.wait_ge(S.sent, 16 * len(others))

@@ -3,28 +3,12 @@ SCRATCH = {
     "pack": ("sbuf", [128, 1024], "float32"),
     "out": ("sbuf", [128, 1061], "float32"),
 }
-SEMAPHORES = ["ld", "pk0", "pk1", "pk2", "pk3", "gp0", "gp1", "gp2", "gp3", "arr", "sent", "st"]
+SEMAPHORES = ["lda", "ldb", "xin", "pk0", "pk1", "pk2", "pk3", "gp0", "gp1", "gp2", "gp3", "arr", "sent", "st"]
 
 
-def plan(tables):
-    route, cap, n = tables["ROUTE"], tables["CAP"], len(tables["ROUTE"])
-    fill = [0] * n
-    kept = [[[] for _e in range(n)] for _r in range(n)]
-    off = [[0] * n for _r in range(n)]
-    for r in range(n):
-        for e in range(n):
-            off[r][e] = min(fill[e], cap)
-        for t, experts in enumerate(route[r]):
-            for e in experts:
-                if fill[e] < cap:
-                    kept[r][e].append(t)
-                fill[e] += 1
-    return kept, off, [min(f, cap) for f in fill]
-
-
-def runs_of(tokens):
+def runs_of(cols):
     runs = []
-    for pos, t in enumerate(tokens):
+    for pos, (t, _c) in enumerate(cols):
         if runs and runs[-1][0] + runs[-1][1] == t:
             runs[-1][1] += 1
         else:
@@ -32,61 +16,98 @@ def runs_of(tokens):
     return runs
 
 
+def plan(tables):
+    route, cap, n = tables["ROUTE"], tables["CAP"], len(tables["ROUTE"])
+    fill = [0] * n
+    kept = [[[] for _e in range(n)] for _r in range(n)]
+    for r in range(n):
+        for t, experts in enumerate(route[r]):
+            for e in experts:
+                if fill[e] < cap:
+                    kept[r][e].append((t, fill[e]))
+                fill[e] += 1
+    part, split = [], []
+    for r in range(n):
+        best = None
+        for h in range(2, len(route[r]) - 1):
+            two = [[[p for p in kept[r][e] if (p[0] >= h) == (w == 1)] for e in range(n)] for w in (0, 1)]
+            load = max(sum(len(runs_of(b)) for b in w) for w in two)
+            if best is None or load < best[0]:
+                best = (load, h, two)
+        split.append(best[1])
+        part.append(best[2])
+    return part, split, [min(f, cap) for f in fill]
+
+
+def helper_of(T, topo, rank):
+    idle = [c for c in range(8 * topo.chip(T.cores[0]), 8 * topo.chip(T.cores[0]) + 8) if c not in T.cores]
+    return idle[rank]
+
+
 def rank_program(g, core, T, topo):
-    rank = T.rank_of(core)
-    if rank is None:
-        return
-    kept, off, count = plan(T.tables)
     n = len(T.cores)
+    rank, worker = T.rank_of(core), 0
+    if rank is None:
+        served = [r for r in range(n) if helper_of(T, topo, r) == core]
+        if not served:
+            return
+        rank, worker = served[0], 1
+    part, split, count = plan(T.tables)
+    blocks, h, width = part[rank][worker], split[rank], T.xs.shape[1]
     S = T.sem
     queues = [g.sync, g.scalar, g]
+    sends = 0
 
-    g.sync.dma_start(T.xs[:], T.x[:]).then_inc(S.ld, 16)
+    def write(dst, out_ap, in_ap, sem):
+        rid, pid, _se = topo.addr(dst)
+        g.remote_dma(out_ap, in_ap, sem, S.sent, pid, rid, topo.mask(core, dst))
+
+    if worker == 0:
+        g.sync.dma_start(T.xs[:, h:width], T.x[:, h:width]).then_inc(S.ldb, 16)
+        g.scalar.dma_start(T.xs[:, 0:h], T.x[:, 0:h]).then_inc(S.lda, 16)
+        g.wait_ge(S.ldb, 16)
+        write(helper_of(T, topo, rank), T.xs[:, h:width], T.xs[:, h:width], S.xin)
+        sends += 1
     for q in queues:
-        q.wait_ge(S.ld, 16)
+        q.wait_ge(S.lda if worker == 0 else S.xin, 16)
 
-    others = sorted((e for e in range(n) if e != rank and kept[rank][e]), key=lambda e: -len(kept[rank][e]))
-    order = others + ([rank] if kept[rank][rank] else [])
+    mine = rank if worker == 0 else None
+    others = sorted((e for e in range(n) if e != mine and blocks[e]), key=lambda e: -len(blocks[e]))
+    order = others + ([mine] if mine is not None and blocks[mine] else [])
     place, base = {}, 0
-    for e in others:
-        place[e] = (T.pack, base)
-        base += len(kept[rank][e])
-    place[rank] = (T.out, off[rank][rank])
+    for e in order:
+        if e == mine:
+            place[e] = (T.out, blocks[e][0][1])
+        else:
+            place[e] = (T.pack, base)
+            base += len(blocks[e])
 
-    share = {e: [runs_of(kept[rank][e])[k::3] for k in range(3)] for e in order}
-
-    def issue(k, e):
+    todo = [(e, run) for e in order for run in runs_of(blocks[e])]
+    cut = (2 * len(todo) + 2) // 3
+    issued = {e: [0, 0] for e in order}
+    for i, (e, (t, ln, pos)) in enumerate(todo):
+        soft = i >= cut
+        q = g if soft else queues[i % 2]
         buf, b = place[e]
-        sem = S["gp%d" % e] if k == 2 else S["pk%d" % e]
-        for t, ln, pos in share[e][k]:
-            queues[k].dma_start(buf[:, b + pos:b + pos + ln], T.xs[:, t:t + ln]).then_inc(sem, 16)
+        q.dma_start(buf[:, b + pos:b + pos + ln], T.xs[:, t:t + ln]).then_inc(S[("gp%d" if soft else "pk%d") % e], 16)
+        issued[e][1 if soft else 0] += 1
 
-    for k in (0, 1):
-        for e in order:
-            issue(k, e)
+    for e in order:
+        if issued[e][0]:
+            g.wait_ge(S["pk%d" % e], 16 * issued[e][0])
+        if issued[e][1]:
+            g.wait_ge(S["gp%d" % e], 16 * issued[e][1])
+        if e != mine:
+            b, w, col = place[e][1], len(blocks[e]), blocks[e][0][1]
+            write(T.cores[e], T.out[:, col:col + w], T.pack[:, b:b + w], S.arr)
+            sends += 1
 
-    if order:
-        issue(2, order[0])
-    for i, e in enumerate(order):
-        if i + 1 < len(order):
-            issue(2, order[i + 1])
-        hw = len(share[e][0]) + len(share[e][1])
-        if hw:
-            g.wait_ge(S["pk%d" % e], 16 * hw)
-        if share[e][2]:
-            g.wait_ge(S["gp%d" % e], 16 * len(share[e][2]))
-        if e != rank:
-            dst = T.cores[e]
-            rid, pid, _se = topo.addr(dst)
-            b, w = place[e][1], len(kept[rank][e])
-            g.remote_dma(T.out[:, off[rank][e]:off[rank][e] + w], T.pack[:, b:b + w], S.arr, S.sent,
-                         pid, rid, topo.mask(core, dst))
-
-    senders = sum(1 for r in range(n) if r != rank and kept[r][rank])
-    if senders:
-        g.wait_ge(S.arr, 16 * senders)
-    if count[rank]:
-        g.dma_start(T.y[:, 0:count[rank]], T.out[:, 0:count[rank]]).then_inc(S.st, 16)
-        g.wait_ge(S.st, 16)
-    if others:
-        g.wait_ge(S.sent, 16 * len(others))
+    if worker == 0:
+        landing = sum(1 for r in range(n) for w in (0, 1) if (r, w) != (rank, 0) and part[r][w][rank])
+        if landing:
+            g.wait_ge(S.arr, 16 * landing)
+        if count[rank]:
+            g.dma_start(T.y[:, 0:count[rank]], T.out[:, 0:count[rank]]).then_inc(S.st, 16)
+            g.wait_ge(S.st, 16)
+    if sends:
+        g.wait_ge(S.sent, 16 * sends)

SCRATCH = {
    "xs": ("sbuf", [128, 512], "float32"),
    "pack": ("sbuf", [128, 1024], "float32"),
    "out": ("sbuf", [128, 1061], "float32"),
}
SEMAPHORES = ["lda", "ldb", "xin", "pk0", "pk1", "pk2", "pk3", "gp0", "gp1", "gp2", "gp3", "arr", "sent", "st"]


def runs_of(cols):
    runs = []
    for pos, (t, _c) in enumerate(cols):
        if runs and runs[-1][0] + runs[-1][1] == t:
            runs[-1][1] += 1
        else:
            runs.append([t, 1, pos])
    return runs


def plan(tables):
    route, cap, n = tables["ROUTE"], tables["CAP"], len(tables["ROUTE"])
    fill = [0] * n
    kept = [[[] for _e in range(n)] for _r in range(n)]
    for r in range(n):
        for t, experts in enumerate(route[r]):
            for e in experts:
                if fill[e] < cap:
                    kept[r][e].append((t, fill[e]))
                fill[e] += 1
    part, split = [], []
    for r in range(n):
        best = None
        for h in range(2, len(route[r]) - 1):
            two = [[[p for p in kept[r][e] if (p[0] >= h) == (w == 1)] for e in range(n)] for w in (0, 1)]
            load = max(sum(len(runs_of(b)) for b in w) for w in two)
            if best is None or load < best[0]:
                best = (load, h, two)
        split.append(best[1])
        part.append(best[2])
    return part, split, [min(f, cap) for f in fill]


def helper_of(T, topo, rank):
    idle = [c for c in range(8 * topo.chip(T.cores[0]), 8 * topo.chip(T.cores[0]) + 8) if c not in T.cores]
    return idle[rank]


def rank_program(g, core, T, topo):
    n = len(T.cores)
    rank, worker = T.rank_of(core), 0
    if rank is None:
        served = [r for r in range(n) if helper_of(T, topo, r) == core]
        if not served:
            return
        rank, worker = served[0], 1
    part, split, count = plan(T.tables)
    blocks, h, width = part[rank][worker], split[rank], T.xs.shape[1]
    S = T.sem
    queues = [g.sync, g.scalar, g]
    sends = 0

    def write(dst, out_ap, in_ap, sem):
        rid, pid, _se = topo.addr(dst)
        g.remote_dma(out_ap, in_ap, sem, S.sent, pid, rid, topo.mask(core, dst))

    if worker == 0:
        g.sync.dma_start(T.xs[:, h:width], T.x[:, h:width]).then_inc(S.ldb, 16)
        g.scalar.dma_start(T.xs[:, 0:h], T.x[:, 0:h]).then_inc(S.lda, 16)
        g.wait_ge(S.ldb, 16)
        write(helper_of(T, topo, rank), T.xs[:, h:width], T.xs[:, h:width], S.xin)
        sends += 1
    for q in queues:
        q.wait_ge(S.lda if worker == 0 else S.xin, 16)

    mine = rank if worker == 0 else None
    others = sorted((e for e in range(n) if e != mine and blocks[e]), key=lambda e: -len(blocks[e]))
    order = others + ([mine] if mine is not None and blocks[mine] else [])
    place, base = {}, 0
    for e in order:
        if e == mine:
            place[e] = (T.out, blocks[e][0][1])
        else:
            place[e] = (T.pack, base)
            base += len(blocks[e])

    todo = [(e, run) for e in order for run in runs_of(blocks[e])]
    cut = (2 * len(todo) + 2) // 3
    issued = {e: [0, 0] for e in order}
    for i, (e, (t, ln, pos)) in enumerate(todo):
        soft = i >= cut
        q = g if soft else queues[i % 2]
        buf, b = place[e]
        q.dma_start(buf[:, b + pos:b + pos + ln], T.xs[:, t:t + ln]).then_inc(S[("gp%d" if soft else "pk%d") % e], 16)
        issued[e][1 if soft else 0] += 1

    for e in order:
        if issued[e][0]:
            g.wait_ge(S["pk%d" % e], 16 * issued[e][0])
        if issued[e][1]:
            g.wait_ge(S["gp%d" % e], 16 * issued[e][1])
        if e != mine:
            b, w, col = place[e][1], len(blocks[e]), blocks[e][0][1]
            write(T.cores[e], T.out[:, col:col + w], T.pack[:, b:b + w], S.arr)
            sends += 1

    if worker == 0:
        landing = sum(1 for r in range(n) for w in (0, 1) if (r, w) != (rank, 0) and part[r][w][rank])
        if landing:
            g.wait_ge(S.arr, 16 * landing)
        if count[rank]:
            g.dma_start(T.y[:, 0:count[rank]], T.out[:, 0:count[rank]]).then_inc(S.st, 16)
            g.wait_ge(S.st, 16)
    if sends:
        g.wait_ge(S.sent, 16 * sends)
